import numpy as np
import ml_dtypes


def mxq(x, axis, fmt="e4m3"):
    dtype, down = {"e4m3": (ml_dtypes.float8_e4m3fn, 7), "e5m2": (ml_dtypes.float8_e5m2, 14)}[fmt]
    v = np.moveaxis(np.asarray(x, np.float32).astype(ml_dtypes.bfloat16).astype(np.float64), axis, -1)
    blocks = v.reshape(v.shape[:-1] + (-1, 32))
    amax = np.abs(blocks).max(-1, keepdims=True)
    byte = np.maximum(np.where(amax > 0, np.frexp(amax)[1] - 1 + 127, 0) - down, 1)
    scale = np.exp2(byte - 127.0)
    codes = (blocks / scale).astype(np.float32).astype(dtype).astype(np.float64)
    return np.moveaxis((codes * scale).reshape(v.shape), -1, axis)


WIDE = False


def mx_kscale(k):
    if not WIDE:
        return np.ones(k)
    levels = np.array([10, -10, 5, -5, 0])
    if k % 512:
        return np.exp2(np.random.permutation(np.resize(levels, k // 32))).repeat(32)
    a = np.empty((k // 512, 16))
    for p in range(k // 512):
        a[p, :8] = np.random.permutation(np.resize(levels, 8))
        for g in range(8):
            far = levels[np.abs(levels - a[p, g]) >= 10]
            a[p, g + 8] = far[np.random.randint(len(far))]
    return np.exp2(a.ravel()).repeat(32)


def f64(x):
    return np.asarray(x).astype(np.float64)


def striped(idx):
    return np.tile(np.asarray(idx).reshape(-1, 16).T, (8, 1)).astype(np.uint16)


def unstriped(offs):
    return offs[:16].T.reshape(-1).astype(np.int64)


G, K, T, D, M = 256, 16, 2048, 512, 512


def setup_inputs():
    n = np.random.standard_normal
    s = mx_kscale(D)[:, None]
    grid = lambda x: np.round(x * 32) / 32
    x = grid(n((D, T))) * s
    idx = np.random.randint(0, T, (G, K))
    part = np.random.randint(1, 128 // K, (G, K)) / 64.0
    return {
        "xT": x.astype(np.float32),
        "w": (n((D, M)) / np.sqrt(D) / s).astype(np.float32),
        "part": np.tile(part.reshape(-1), (128, 1)).astype(np.float32),
        "offs": striped(idx.reshape(-1)),
    }


def reference(xT, w, part, offs):
    x = f64(xT)[:, unstriped(offs)]
    y = mxq(f64(w), 0, "e4m3").T @ mxq((x * f64(part)[:1]).reshape(D, G, K).sum(-1), 0, "e4m3")
    return y

from contextlib import ExitStack

import concourse.mybir as mybir
from concourse.masks import make_identity

P = 128
D, T, M, G, K = 512, 2048, 512, 256, 16
ENTRIES = G * K
FLOPS = 2 * D * M * G
BYTES = D * T * 4 + D * M * 4 + ENTRIES * 4 + P * (ENTRIES // 16) * 2 + M * G * 4

F32 = mybir.dt.float32
BF16 = mybir.dt.bfloat16
U32 = mybir.dt.uint32
U16 = mybir.dt.uint16
U8 = mybir.dt.uint8
FP8X4 = mybir.dt.float8_e4m3fn_x4
COPY = mybir.ActivationFunctionType.Copy
MULT = mybir.AluOpType.mult
ADD = mybir.AluOpType.add

COLS = 512
UNIT = 512
UNITS = ENTRIES // UNIT
VEC_UNITS = {(1, 6), (1, 7)}


def tile_attend_grid_kernel(tc, xT, w, part, offs, out):
    nc = tc.nc
    x_view = xT.rearrange("(p j) c -> p j c", j=4)
    with ExitStack() as ctx:
        held = ctx.enter_context(tc.tile_pool(name="held", bufs=1))
        work = ctx.enter_context(tc.tile_pool(name="work", bufs=3))
        fpsum = ctx.enter_context(tc.psum_pool(name="fpsum", bufs=3))
        bpsum = ctx.enter_context(tc.psum_pool(name="bpsum", bufs=3))
        mpsum = ctx.enter_context(tc.psum_pool(name="mpsum", bufs=2))

        offsets = held.tile([P, ENTRIES // 16], U16)
        raw = {}

        def load(u, k):
            t = held.tile([P, 2, COLS], F32, name="raw%d_%d" % (u, k))
            nc.sync.dma_start(out=t[:], in_=x_view[:, 2 * u : 2 * u + 2, k * COLS : (k + 1) * COLS])
            raw[(u, k)] = t

        part_rows = held.tile([P, 256], F32)
        w_raw = held.tile([P, 4, M], F32)
        load(0, 0)
        nc.sync.dma_start(offsets[:], offs)
        for k in range(1, T // COLS):
            load(0, k)
        nc.scalar.dma_start(out=part_rows[:], in_=part[0:8, :].rearrange("a (c r) -> (a c) r", r=256))
        nc.sync.dma_start(out=w_raw[:], in_=w.rearrange("(p j) m -> p j m", j=4))
        for k in range(T // COLS):
            load(1, k)

        ident = held.tile([P, P], F32)
        make_identity(nc, ident[:])

        factors = held.tile([P, 2, 16], F32)
        fbank = fpsum.tile([P, 4, P], F32, name="fwd")
        for h in range(2):
            nc.tensor.transpose(fbank[:, h, :], part_rows[:, h : 256 : 2], ident[:])
        nc.scalar.copy(out=factors[:], in_=fbank[:, 0:2, 0:16])

        window = []
        for u in range(2):
            win = held.tile([P, 2 * T], BF16, name="win%d" % u)
            window.append(win)

        def widen(u, k):
            dst = window[u][:].rearrange("p (c e) -> p c e", e=2)[:, k * COLS : (k + 1) * COLS, :]
            src = raw[(u, k)][:].rearrange("p e c -> p c e")
            if u == 0:
                nc.vector.tensor_copy(out=dst, in_=src)
            else:
                nc.scalar.activation(out=dst, in_=src, func=COPY)

        for k in range(T // COLS):
            widen(0, k)

        w_bf = held.tile([P, M, 4], BF16, align_bytes=64)
        w_codes = held.tile([P, M], U32, align_bytes=64)
        w_scales = held.tile([P, M], U8, align_bytes=64)
        nc.gpsimd.tensor_scalar(out=w_bf[:], in0=w_raw[:].rearrange("p j m -> p m j"), scalar1=1.0, scalar2=0.0, op0=MULT, op1=ADD)

        e_bf = []
        for b in range(2):
            eb = held.tile([P, G // 2, 4], BF16, name="e%d" % b, align_bytes=64)
            e_bf.append(eb)

        gathered = {}

        def gather(u, q0, n):
            g = work.tile([P, 1024], U32, name="gathered", bufs=3)
            c0 = q0 * UNIT // 16
            nc.vector.tensor_copy(out=g[:, 0 : n * UNIT], in_=window[u][:].bitcast(U32).indirect(offsets[:, c0 : c0 + n * UNIT // 16]))
            for q in range(n):
                gathered[(u, q0 + q)] = (g, q * UNIT)

        summed = {}

        def weigh(u, q):
            g, base = gathered[(u, q)]
            bank = fpsum.tile([P, 4, P], F32, name="fwd")
            for c in range(2):
                for h in range(2):
                    a = base + 256 * c
                    nc.tensor.transpose(bank[:, 2 * c + h, :], g[:, a + h : a + 256 : 2].bitcast(F32), ident[:])
            prod = work.tile([P, 2, 2, 2, P], F32, name="prod")
            sums = work.tile([P, 2, 2, P], F32, name="sums")
            on_vector = (u, q) in VEC_UNITS
            for c in range(2):
                for h in range(2):
                    src = bank[:, 2 * c + h, :].bitcast(BF16).rearrange("r (p e) -> r e p", e=2)
                    factor = factors[:, h, 2 * q + c : 2 * q + c + 1]
                    if h == 0 or not on_vector:
                        nc.scalar.activation(out=prod[:, h, c], in_=src, func=COPY, scale=factor)
                    else:
                        nc.vector.scalar_tensor_tensor(out=sums[:, c], in0=src, scalar=factor, in1=prod[:, 0, c], op0=MULT, op1=ADD)
            if not on_vector:
                nc.gpsimd.tensor_tensor(out=sums[:], in0=prod[:, 0], in1=prod[:, 1], op=ADD)
            summed[(u, q)] = sums

        def collect(u, q):
            sums = summed[(u, q)]
            bank = bpsum.tile([P, 2, 2, P], F32, name="back")
            for c in range(2):
                for e in range(2):
                    nc.tensor.transpose(bank[:, e, c, :], sums[:, c, e, :], ident[:])
            g0 = 32 * (q % 4)
            with nc.allow_low_precision(reason="sums in float32, one rounding to bfloat16 at the end"):
                nc.vector.tensor_reduce(
                    out=e_bf[q // 4][:, g0 : g0 + 32, 2 * u : 2 * u + 2],
                    in_=bank[:].rearrange("p e c (g j) -> p (c g) e j", j=8),
                    axis=mybir.AxisListType.X,
                    op=ADD,
                )

        out_view = out.rearrange("(t p) g -> p t g", p=P)

        def layer(b):
            codes = work.tile([P, G // 2], U32, name="codes", bufs=2, align_bytes=64)
            scales = work.tile([P, G // 2], U8, name="scales", bufs=2, align_bytes=64)
            nc.vector.quantize_mx(out=codes[:].bitcast(FP8X4), scales=scales[:], in_=e_bf[b][:].rearrange("p g t -> p (g t)"))
            for s in range(2):
                bank = mpsum.tile([P, 2, G // 2], F32, name="mx")
                for i in range(2):
                    cols = slice((2 * s + i) * P, (2 * s + i + 1) * P)
                    nc.tensor.matmul_mx(out=bank[:, i, :], lhsT=w_codes[:, cols].bitcast(FP8X4), lhsT_scale=w_scales[:, cols],
                                        rhs=codes[:].bitcast(FP8X4), rhs_scale=scales[:], start=True, stop=True)
                y = work.tile([P, 2, G // 2], F32, name="y", bufs=4)
                if s == 0 or b == 0:
                    nc.scalar.copy(out=y[:], in_=bank[:])
                else:
                    nc.vector.tensor_copy(out=y[:], in_=bank[:])
                nc.sync.dma_start(out=out_view[:, 2 * s : 2 * s + 2, b * (G // 2) : (b + 1) * (G // 2)], in_=y[:])

        units = []
        for u in range(2):
            for q in range(UNITS):
                units.append((u, q))
        pieces = [(0, 0, 1), (0, 1, 1), (0, 2, 2), (0, 4, 2), (0, 6, 2), (1, 0, 2), (1, 2, 2), (1, 4, 2), (1, 6, 1), (1, 7, 1)]
        starts = {}
        for u, q0, n in pieces:
            starts[(u, q0)] = n
        order = []
        for u, q0, n in pieces:
            for q in range(n):
                order.append((u, q0 + q))

        lag = 2
        done = []
        gi = 0
        have = 0
        for s in range(len(order) + lag):
            while gi < len(pieces) and have < s + 2 + 0:
                gather(pieces[gi][0], pieces[gi][1], pieces[gi][2])
                have += pieces[gi][2]
                gi += 1
                if gi == 1:
                    for k in range(T // COLS):
                        widen(1, k)
                if gi == 4:
                    nc.vector.quantize_mx(out=w_codes[:].bitcast(FP8X4), scales=w_scales[:], in_=w_bf[:].rearrange("p m j -> p (m j)"))
            if s < len(order):
                weigh(order[s][0], order[s][1])
            if s >= lag:
                u, q = order[s - lag]
                collect(u, q)
                done.append((u, q))
                b = q // 4
                if len([x for x in done if x[1] // 4 == b]) == 8:
                    layer(b)
